import numpy as np
import ml_dtypes


def mxq(x, axis, fmt="e4m3"):
    dtype, down = {"e4m3": (ml_dtypes.float8_e4m3fn, 7), "e5m2": (ml_dtypes.float8_e5m2, 14)}[fmt]
    v = np.moveaxis(np.asarray(x, np.float32).astype(ml_dtypes.bfloat16).astype(np.float64), axis, -1)
    blocks = v.reshape(v.shape[:-1] + (-1, 32))
    amax = np.abs(blocks).max(-1, keepdims=True)
    byte = np.maximum(np.where(amax > 0, np.frexp(amax)[1] - 1 + 127, 0) - down, 1)
    scale = np.exp2(byte - 127.0)
    codes = (blocks / scale).astype(np.float32).astype(dtype).astype(np.float64)
    return np.moveaxis((codes * scale).reshape(v.shape), -1, axis)


WIDE = False


def mx_kscale(k):
    if not WIDE:
        return np.ones(k)
    levels = np.array([10, -10, 5, -5, 0])
    if k % 512:
        return np.exp2(np.random.permutation(np.resize(levels, k // 32))).repeat(32)
    a = np.empty((k // 512, 16))
    for p in range(k // 512):
        a[p, :8] = np.random.permutation(np.resize(levels, 8))
        for g in range(8):
            far = levels[np.abs(levels - a[p, g]) >= 10]
            a[p, g + 8] = far[np.random.randint(len(far))]
    return np.exp2(a.ravel()).repeat(32)


def f64(x):
    return np.asarray(x).astype(np.float64)


def striped(idx):
    return np.tile(idx.reshape(-1, 16).T, (8, 1)).astype(np.uint16)


def unstriped(offs):
    return offs[:16].T.reshape(-1).astype(np.int64)


E2M1 = np.array([0.0, 0.5, 1.0, 1.5, 2.0, 3.0, 4.0, 6.0, -0.0, -0.5, -1.0, -1.5, -2.0, -3.0, -4.0, -6.0])


def pack_weight(w, fmt):
    k, n = w.shape
    w = f64(np.asarray(w, np.float32).astype(ml_dtypes.bfloat16)).reshape(k // 32, 32, n)
    amax = np.abs(w).max(1)
    if fmt == "e4m3":
        byte = np.frexp(amax)[1] - 1 + 127 - 7
    else:
        mant, ex = np.frexp(amax / 6.0)
        byte = np.where(mant > 0.5, ex, ex - 1) + 127
    byte = np.clip(np.where(amax > 0, byte, 1), 1, 254)
    scaled = (w * np.exp2(127.0 - byte)[:, None, :]).reshape(k, n).astype(np.float32)
    by_word = np.ascontiguousarray(scaled.reshape(k // 512, 128, 4, n).transpose(0, 1, 3, 2))
    if fmt == "e4m3":
        words = by_word.astype(ml_dtypes.float8_e4m3fn).view(np.uint8)
    else:
        c = by_word.astype(ml_dtypes.float4_e2m1fn).view(np.uint8) & 0xF
        words = (c[..., 0::2] | (c[..., 1::2] << 4)).reshape(k // 512, 128, 2 * n)
    return np.ascontiguousarray(words), np.ascontiguousarray(byte.astype(np.uint8).reshape(k // 512, 16, n))


def unpack_weight(words, scales, fmt):
    g, _, n = scales.shape
    words = np.ascontiguousarray(words).reshape(g, 128, n, -1)
    if fmt == "e4m3":
        vals = words.view(ml_dtypes.float8_e4m3fn).astype(np.float64)
    else:
        nib = np.empty((g, 128, n, 4), np.uint8)
        nib[..., 0::2] = words & 0xF
        nib[..., 1::2] = words >> 4
        vals = E2M1[nib]
    vals = vals * np.repeat(np.exp2(scales.astype(np.float64) - 127.0), 8, axis=1)[..., None]
    return vals.transpose(0, 1, 3, 2).reshape(g * 512, n)


def gelu(v):
    return 0.5 * v * (1.0 + np.tanh(np.sqrt(2.0 / np.pi) * (v + 0.044715 * v**3)))


def striped8(idx):
    return np.concatenate([v.reshape(-1, 16).T for v in idx]).astype(np.uint16)


def unstriped8(offs):
    return np.stack([offs[16 * g:16 * g + 16].T.reshape(-1) for g in range(8)]).astype(np.int64)


def heads(h, wgt, idx8):
    r = np.arange(h.shape[0])
    return wgt[r // 4 % 128] * h[r[:, None], idx8[r % 512 // 64]]


K, T, S, P, H, N = 1024, 4096, 1024, 512, 1024, 512

def setup_inputs():
    n = np.random.standard_normal
    s = mx_kscale(K)[:, None]
    u = mx_kscale(H)[:, None]
    tab_words, tab_scales = pack_weight(n((K, T)) * s, "e4m3")
    w4_words, w4_scales = pack_weight(n((K, H)) / np.sqrt(K) / s, "e2m1")
    return {
        "tab_words": tab_words, "tab_scales": tab_scales,
        "offs": striped(np.random.permutation(T)[:S]),
        "w4_words": w4_words, "w4_scales": w4_scales,
        "plot": n((H, S)).astype(np.float32),
        "gain": (np.sign(n(H)) * np.exp(0.3 * n(H)) * u[:, 0]).astype(np.float32),
        "offs2": striped8(np.stack([np.random.permutation(S)[:P] for _ in range(8)])),
        "wga": np.repeat(np.random.uniform(0.5, 2.0, (8, P)), 16, axis=0).astype(np.float32),
        "offs3": striped8(np.stack([np.random.permutation(S)[:P] for _ in range(8)])),
        "wgb": np.repeat(np.random.uniform(0.5, 2.0, (8, P)), 16, axis=0).astype(np.float32),
        "gv": np.exp(0.4 * n(H)).astype(np.float32),
        "w2": (n((H, N)) / np.sqrt(H) / u).astype(np.float32),
    }

def reference(tab_words, tab_scales, offs, w4_words, w4_scales, plot, gain, offs2, wga, offs3, wgb, gv, w2):
    v = unpack_weight(tab_words, tab_scales, "e4m3")[:, unstriped(offs)]
    w4 = unpack_weight(w4_words, w4_scales, "e2m1")
    h = np.tanh((w4.T @ v) + f64(plot)) * f64(gain)[:, None]
    xa = heads(h, f64(wga), unstriped8(offs2))
    xb = heads(h, f64(wgb), unstriped8(offs3))
    x = np.minimum(xa, xb) * f64(gv)[:, None]
    out = mxq(f64(w2), 0, "e4m3").T @ mxq(x, 0, "e4m3")
    return out

@@ -1,0 +1,189 @@
+from contextlib import ExitStack
+
+import concourse.mybir as mybir
+
+K, T, S, M, H, N = 1024, 4096, 1024, 512, 1024, 512
+FLOPS = 2 * K * H * S + 2 * H * N * M
+
+F32 = mybir.dt.float32
+BF16 = mybir.dt.bfloat16
+I32 = mybir.dt.int32
+U32 = mybir.dt.uint32
+U16 = mybir.dt.uint16
+U8 = mybir.dt.uint8
+FP8X4 = mybir.dt.float8_e4m3fn_x4
+FP4X4 = mybir.dt.float4_e2m1fn_x4
+ALU = mybir.AluOpType
+ACT = mybir.ActivationFunctionType
+
+P = 128
+PACK = 4
+BANK = 512
+CHUNKS = ((0, 256), (256, 128), (384, 128))
+
+
+def tile_list_barley_duplicate_overlap_kernel(
+    tc, tab_words, tab_scales, offs, w4_words, w4_scales, plot, gain, offs2, wga, offs3, wgb, gv, w2, out
+):
+    nc = tc.nc
+    with ExitStack() as ctx:
+        keep = ctx.enter_context(tc.tile_pool(name="keep", bufs=1))
+        ring = ctx.enter_context(tc.tile_pool(name="ring", bufs=2))
+        psum = ctx.enter_context(tc.psum_pool(name="psum", bufs=1))
+
+        list1 = keep.tile([P, S // 16], U16, name="list1")
+        list2 = keep.tile([P, M // 16], U16, name="list2")
+        list3 = keep.tile([P, M // 16], U16, name="list3")
+        tab_w = [keep.tile([P, T], U32, name="tab_w%d" % a, align_bytes=64) for a in range(2)]
+        tab_s = keep.tile([P, T], U8, name="tab_s", align_bytes=64)
+        v_w = [[keep.tile([P, BANK], U32, name="v_w%d%d" % (a, c), align_bytes=64) for c in range(2)] for a in range(2)]
+        v_s = [keep.tile([P, S], U8, name="v_s%d" % a, align_bytes=64) for a in range(2)]
+        w4_raw = keep.tile([P, 2, 2 * H], U8, name="w4_raw", align_bytes=64)
+        w4_w = keep.tile([P, 2, 2 * H], U8, name="w4_w", align_bytes=64)
+        w4s_raw = keep.tile([P, 2, H], U8, name="w4s_raw", align_bytes=64)
+        w4_s = keep.tile([P, 2, H], U8, name="w4_s", align_bytes=64)
+        gain_t = keep.tile([P, 2, PACK], F32, name="gain_t")
+        gv_t = keep.tile([P, 2, PACK], F32, name="gv_t")
+        wga_t = keep.tile([P, M], F32, name="wga_t", align_bytes=64)
+        wgb_t = keep.tile([P, M], F32, name="wgb_t", align_bytes=64)
+        z = [keep.tile([P, S], F32, name="z%d" % t, align_bytes=64) for t in range(8)]
+        h = [keep.tile([P, S], F32, name="h%d" % t, align_bytes=64) for t in range(8)]
+        w2_raw = [keep.tile([P, PACK, N], F32, name="w2_raw%d" % b, align_bytes=64) for b in range(2)]
+        w2_w = [keep.tile([P, N], U32, name="w2_w%d" % b, align_bytes=64) for b in range(2)]
+        w2_s = [keep.tile([P, N], U8, name="w2_s%d" % b, align_bytes=64) for b in range(2)]
+        x_w = [keep.tile([P, M], U32, name="x_w%d" % b, align_bytes=64) for b in range(2)]
+        x_s = [keep.tile([P, M], U8, name="x_s%d" % b, align_bytes=64) for b in range(2)]
+
+        nc.vector.memset(tab_s[:].bitcast(I32), 0)
+        nc.vector.memset(w4s_raw[:].rearrange("p a c -> p (a c)").bitcast(I32), 0)
+        nc.vector.memset(v_s[1][:].bitcast(I32), 0)
+
+        nc.sync.dma_start(list1[:], offs)
+        for q in range(4):
+            nc.scalar.dma_start(tab_s[32 * q : 32 * q + 8, :].bitcast(I32), tab_scales[:, 4 * q : 4 * q + 4, :].bitcast(I32))
+        nc.sync.dma_start(tab_w[0][:].bitcast(I32), tab_words[0].rearrange("p t i -> p (t i)").bitcast(I32))
+        nc.sync.dma_start(w4_raw[:].bitcast(I32), w4_words.rearrange("a p c -> p a c").bitcast(I32))
+        nc.sync.dma_start(tab_w[1][:].bitcast(I32), tab_words[1].rearrange("p t i -> p (t i)").bitcast(I32))
+        for q in range(4):
+            nc.scalar.dma_start(
+                w4s_raw[32 * q : 32 * q + 4, :, :].bitcast(I32),
+                w4_scales[:, 4 * q : 4 * q + 4, :].rearrange("a r c -> r a c").bitcast(I32),
+            )
+        nc.gpsimd.dma_start(gain_t[:], gain.rearrange("(b p i) -> p b i", b=2, i=PACK))
+        nc.gpsimd.dma_start(gv_t[:], gv.rearrange("(b p i) -> p b i", b=2, i=PACK))
+        plot_rows = plot.rearrange("(b p i) j -> b i p j", b=2, i=PACK)
+        nc.sync.dma_start(z[0][:], plot_rows[0, 0])
+        nc.sync.dma_start(list2[:], offs2)
+        nc.sync.dma_start(list3[:], offs3)
+        nc.sync.dma_start(wga_t[:], wga)
+        nc.sync.dma_start(wgb_t[:], wgb)
+        for t in range(1, 8):
+            nc.sync.dma_start(z[t][:], plot_rows[t // PACK, t % PACK])
+        for b in range(2):
+            nc.sync.dma_start(w2_raw[b][:], w2[512 * b : 512 * (b + 1), :].rearrange("(p i) n -> p i n", i=PACK))
+
+        nc.vector.tensor_copy(v_s[0][:], tab_s[:].indirect(list1[:]))
+        nc.scalar.dma_start(v_s[1][0:100, :].bitcast(I32), v_s[0][4:104, :].bitcast(I32))
+        for c in range(2):
+            nc.vector.tensor_copy(v_w[0][c][:], tab_w[0][:].indirect(list1[:, 32 * c : 32 * (c + 1)]))
+        nc.vector.tensor_copy(
+            w4_w[:].bitcast(U16).rearrange("p a (b i q) -> p (a b) i q", b=2, i=PACK),
+            w4_raw[:].bitcast(U16).rearrange("p a (b q i) -> p (a b) i q", b=2, i=PACK),
+        )
+        nc.vector.tensor_copy(
+            w4_s[:].rearrange("p a (b i q) -> p (a b) i q", b=2, i=PACK),
+            w4s_raw[:].rearrange("p a (b q i) -> p (a b) i q", b=2, i=PACK),
+        )
+        for c in range(2):
+            nc.vector.tensor_copy(v_w[1][c][:], tab_w[1][:].indirect(list1[:, 32 * c : 32 * (c + 1)]))
+
+        def features(t):
+            for c in range(2):
+                cols = slice(BANK * c, BANK * (c + 1))
+                acc = psum.tile([P, BANK], F32, name="acc", tag="acc", bufs=4)
+                for a in range(2):
+                    nc.tensor.matmul_mx(
+                        out=acc[:],
+                        lhsT=w4_w[:, a, 2 * P * t : 2 * P * (t + 1)].bitcast(FP4X4),
+                        lhsT_scale=w4_s[:, a, P * t : P * (t + 1)],
+                        rhs=v_w[a][c][:].bitcast(FP8X4),
+                        rhs_scale=v_s[a][:, cols],
+                        start=(a == 0),
+                        stop=(a == 1),
+                    )
+                nc.vector.tensor_tensor(z[t][:, cols], acc[:], z[t][:, cols], ALU.add)
+            nc.scalar.activation(z[t][:], z[t][:], ACT.Tanh)
+            nc.scalar.activation(h[t][:], z[t][:], ACT.Copy, scale=gain_t[:, t // PACK, t % PACK : t % PACK + 1])
+
+        def pick(t, m0, w, x_rows, last):
+            b, i = divmod(t, PACK)
+            lists = slice(m0 // 16, (m0 + w) // 16)
+            xa = ring.tile([P, w], F32, name="xa", tag="xa", align_bytes=64)
+            xb = ring.tile([P, w], F32, name="xb", tag="xb", align_bytes=64)
+            lo = ring.tile([P, w], F32, name="lo", tag="lo", align_bytes=64)
+            nc.vector.tensor_tensor(xa[:], h[t][:].indirect(list2[:, lists]), wga_t[:, m0 : m0 + w], ALU.mult)
+            nc.vector.tensor_tensor(xb[:], h[t][:].indirect(list3[:, lists]), wgb_t[:, m0 : m0 + w], ALU.mult)
+            nc.vector.tensor_tensor(lo[:], xa[:], xb[:], ALU.min)
+            if last:
+                nc.vector.tensor_scalar(x_rows[:, i, :], lo[:], gv_t[:, b, i : i + 1], None, ALU.mult)
+            else:
+                nc.scalar.activation(x_rows[:, i, :], lo[:], ACT.Copy, scale=gv_t[:, b, i : i + 1])
+
+        def weave(copy, rows, w, codes, scales):
+            woven = ring.tile([P, w, PACK], BF16, name="woven", tag="woven", align_bytes=64)
+            copy(
+                woven[:].rearrange("p (c j) i -> p c i j", j=4),
+                rows.rearrange("p i (c j) -> p c i j", j=4),
+            )
+            nc.vector.quantize_mx(out=codes.bitcast(FP8X4), scales=scales, in_=woven[:].rearrange("p w i -> p (w i)"))
+
+        banks = {}
+        for m0, w in CHUNKS:
+            per = BANK // w
+            for g in range(4 // per):
+                banks[m0, g] = psum.tile([P, per, w], F32, name="sum%d_%d" % (m0, g))
+
+        def product(b, m0, w):
+            per = BANK // w
+            for n in range(4):
+                g, s = divmod(n, per)
+                nc.tensor.matmul_mx(
+                    out=banks[m0, g][:, s, :],
+                    lhsT=w2_w[b][:, P * n : P * (n + 1)].bitcast(FP8X4),
+                    lhsT_scale=w2_s[b][:, P * n : P * (n + 1)],
+                    rhs=x_w[b][:, m0 : m0 + w].bitcast(FP8X4),
+                    rhs_scale=x_s[b][:, m0 : m0 + w],
+                    start=(b == 0 and s == 0),
+                    stop=(b == 1 and s == per - 1),
+                )
+
+        out_rows = out.rearrange("(n p) m -> p n m", p=P)
+
+        def store(m0, w):
+            per = BANK // w
+            for g in range(4 // per):
+                res = keep.tile([P, per, w], F32, name="res%d_%d" % (m0, g), align_bytes=64)
+                nc.scalar.copy(res[:], banks[m0, g][:])
+                nc.sync.dma_start(out_rows[:, per * g : per * (g + 1), m0 : m0 + w], res[:])
+
+        x0 = keep.tile([P, PACK, M], BF16, name="x0", align_bytes=64)
+        features(0)
+        features(1)
+        for t in range(PACK):
+            features(t + 2)
+            pick(t, 0, M, x0, False)
+        features(6)
+        features(7)
+        weave(nc.scalar.copy, x0[:], M, x_w[0][:], x_s[0][:])
+        for b in range(2):
+            weave(nc.scalar.copy, w2_raw[b][:], N, w2_w[b][:], w2_s[b][:])
+        for m0, w in CHUNKS:
+            product(0, m0, w)
+        for m0, w in CHUNKS:
+            last = m0 == CHUNKS[-1][0]
+            x1 = keep.tile([P, PACK, w], BF16, name="x1_%d" % m0, align_bytes=64)
+            for t in range(PACK, 2 * PACK):
+                pick(t, m0, w, x1, last)
+            weave(nc.vector.tensor_copy if last else nc.scalar.copy, x1[:], w, x_w[1][:, m0 : m0 + w], x_s[1][:, m0 : m0 + w])
+            product(1, m0, w)
+            store(m0, w)

@@ -19,7 +19,9 @@ ACT = mybir.ActivationFunctionType
 P = 128
 PACK = 4
 BANK = 512
-CHUNKS = ((0, 256), (256, 128), (384, 128))
+FIRST = 384
+HELD = 5
+SUMS = ((0, 256, 2), (256, 128, 4), (384, 128, 2))
 
 
 def tile_list_barley_duplicate_overlap_kernel(
@@ -30,77 +32,86 @@ def tile_list_barley_duplicate_overlap_kernel(
         keep = ctx.enter_context(tc.tile_pool(name="keep", bufs=1))
         ring = ctx.enter_context(tc.tile_pool(name="ring", bufs=2))
         psum = ctx.enter_context(tc.psum_pool(name="psum", bufs=1))
+        twice = ctx.enter_context(tc.tile_pool(name="twice", bufs=1))
 
         list1 = keep.tile([P, S // 16], U16, name="list1")
         list2 = keep.tile([P, M // 16], U16, name="list2")
         list3 = keep.tile([P, M // 16], U16, name="list3")
-        tab_w = [keep.tile([P, T], U32, name="tab_w%d" % a, align_bytes=64) for a in range(2)]
-        tab_s = keep.tile([P, T], U8, name="tab_s", align_bytes=64)
+        KB = 1024
+        tab_s = twice.tile([P, T], U8, name="tab_s", offset=0)
+        tab_w = [twice.tile([P, T], U32, name="tab_w%d" % a, offset=at * KB) for a, at in enumerate((38, 4))]
         v_w = [[keep.tile([P, BANK], U32, name="v_w%d%d" % (a, c), align_bytes=64) for c in range(2)] for a in range(2)]
+        v_sg = keep.tile([P, S], U8, name="v_sg", align_bytes=64)
         v_s = [keep.tile([P, S], U8, name="v_s%d" % a, align_bytes=64) for a in range(2)]
-        w4_raw = keep.tile([P, 2, 2 * H], U8, name="w4_raw", align_bytes=64)
-        w4_w = keep.tile([P, 2, 2 * H], U8, name="w4_w", align_bytes=64)
+        w4_raw = twice.tile([P, 2, 2 * H], U8, name="w4_raw", offset=84 * KB)
+        w4_w = twice.tile([P, 2, 2 * H], U8, name="w4_w", offset=45 * KB, align_bytes=64)
         w4s_raw = keep.tile([P, 2, H], U8, name="w4s_raw", align_bytes=64)
-        w4_s = keep.tile([P, 2, H], U8, name="w4_s", align_bytes=64)
-        gain_t = keep.tile([P, 2, PACK], F32, name="gain_t")
-        gv_t = keep.tile([P, 2, PACK], F32, name="gv_t")
-        wga_t = keep.tile([P, M], F32, name="wga_t", align_bytes=64)
-        wgb_t = keep.tile([P, M], F32, name="wgb_t", align_bytes=64)
-        z = [keep.tile([P, S], F32, name="z%d" % t, align_bytes=64) for t in range(8)]
+        w4_s = twice.tile([P, 2, H], U8, name="w4_s", offset=0, align_bytes=64)
+        gain_t = twice.tile([P, 2, PACK], F32, name="gain_t", offset=53 * KB + 64)
+        gv_t = twice.tile([P, 2, PACK], F32, name="gv_t", offset=53 * KB)
+        wga_t = twice.tile([P, M], F32, name="wga_t", offset=49 * KB)
+        wgb_t = twice.tile([P, M], F32, name="wgb_t", offset=51 * KB)
+        z = [twice.tile([P, S], F32, name="z%d" % t, offset=at * KB) for t, at in enumerate((37, 41, 81, 85, 2, 6, 10, 14))]
         h = [keep.tile([P, S], F32, name="h%d" % t, align_bytes=64) for t in range(8)]
-        w2_raw = [keep.tile([P, PACK, N], F32, name="w2_raw%d" % b, align_bytes=64) for b in range(2)]
+        w2_raw = twice.tile([P, 2, PACK, N], F32, name="w2_raw", offset=18 * KB)
         w2_w = [keep.tile([P, N], U32, name="w2_w%d" % b, align_bytes=64) for b in range(2)]
         w2_s = [keep.tile([P, N], U8, name="w2_s%d" % b, align_bytes=64) for b in range(2)]
         x_w = [keep.tile([P, M], U32, name="x_w%d" % b, align_bytes=64) for b in range(2)]
         x_s = [keep.tile([P, M], U8, name="x_s%d" % b, align_bytes=64) for b in range(2)]
 
-        nc.vector.memset(tab_s[:].bitcast(I32), 0)
-        nc.vector.memset(w4s_raw[:].rearrange("p a c -> p (a c)").bitcast(I32), 0)
-        nc.vector.memset(v_s[1][:].bitcast(I32), 0)
-
+        nc.gpsimd.memset(w4s_raw[:].rearrange("p a c -> p (a c)").bitcast(I32), 0)
         nc.sync.dma_start(list1[:], offs)
         for q in range(4):
-            nc.scalar.dma_start(tab_s[32 * q : 32 * q + 8, :].bitcast(I32), tab_scales[:, 4 * q : 4 * q + 4, :].bitcast(I32))
+            nc.sync.dma_start(tab_s[32 * q + 24 : 32 * q + 32, :].bitcast(I32), tab_scales[:, 4 * q : 4 * q + 4, :].bitcast(I32))
         nc.sync.dma_start(tab_w[0][:].bitcast(I32), tab_words[0].rearrange("p t i -> p (t i)").bitcast(I32))
         nc.sync.dma_start(w4_raw[:].bitcast(I32), w4_words.rearrange("a p c -> p a c").bitcast(I32))
-        nc.sync.dma_start(tab_w[1][:].bitcast(I32), tab_words[1].rearrange("p t i -> p (t i)").bitcast(I32))
         for q in range(4):
-            nc.scalar.dma_start(
+            nc.sync.dma_start(
                 w4s_raw[32 * q : 32 * q + 4, :, :].bitcast(I32),
                 w4_scales[:, 4 * q : 4 * q + 4, :].rearrange("a r c -> r a c").bitcast(I32),
             )
-        nc.gpsimd.dma_start(gain_t[:], gain.rearrange("(b p i) -> p b i", b=2, i=PACK))
-        nc.gpsimd.dma_start(gv_t[:], gv.rearrange("(b p i) -> p b i", b=2, i=PACK))
+        nc.sync.dma_start(tab_w[1][:].bitcast(I32), tab_words[1].rearrange("p t i -> p (t i)").bitcast(I32))
         plot_rows = plot.rearrange("(b p i) j -> b i p j", b=2, i=PACK)
-        nc.sync.dma_start(z[0][:], plot_rows[0, 0])
         nc.sync.dma_start(list2[:], offs2)
         nc.sync.dma_start(list3[:], offs3)
-        nc.sync.dma_start(wga_t[:], wga)
-        nc.sync.dma_start(wgb_t[:], wgb)
-        for t in range(1, 8):
-            nc.sync.dma_start(z[t][:], plot_rows[t // PACK, t % PACK])
-        for b in range(2):
-            nc.sync.dma_start(w2_raw[b][:], w2[512 * b : 512 * (b + 1), :].rearrange("(p i) n -> p i n", i=PACK))
 
-        nc.vector.tensor_copy(v_s[0][:], tab_s[:].indirect(list1[:]))
-        nc.scalar.dma_start(v_s[1][0:100, :].bitcast(I32), v_s[0][4:104, :].bitcast(I32))
+        for q in range(4):
+            nc.vector.memset(tab_s[32 * q : 32 * q + 24, :].bitcast(I32), 0)
+        for a in range(2):
+            nc.vector.memset(v_s[a][96:128, :].bitcast(I32), 0)
+
+        nc.vector.tensor_copy(v_sg[:], tab_s[:].indirect(list1[:]))
+        for a in range(2):
+            nc.scalar.dma_start(v_s[a][0:100, :].bitcast(I32), v_sg[24 + 4 * a : 124 + 4 * a, :].bitcast(I32))
         for c in range(2):
             nc.vector.tensor_copy(v_w[0][c][:], tab_w[0][:].indirect(list1[:, 32 * c : 32 * (c + 1)]))
+        for t in range(2):
+            nc.sync.dma_start(z[t][:], plot_rows[t // PACK, t % PACK])
+        nc.sync.dma_start(gain_t[:], gain.rearrange("(b p i) -> p b i", b=2, i=PACK))
+        nc.sync.dma_start(wga_t[:], wga)
+        nc.sync.dma_start(wgb_t[:], wgb)
+        nc.sync.dma_start(gv_t[:], gv.rearrange("(b p i) -> p b i", b=2, i=PACK))
         nc.vector.tensor_copy(
             w4_w[:].bitcast(U16).rearrange("p a (b i q) -> p (a b) i q", b=2, i=PACK),
             w4_raw[:].bitcast(U16).rearrange("p a (b q i) -> p (a b) i q", b=2, i=PACK),
         )
+        for t in range(2, 4):
+            nc.sync.dma_start(z[t][:], plot_rows[t // PACK, t % PACK])
         nc.vector.tensor_copy(
             w4_s[:].rearrange("p a (b i q) -> p (a b) i q", b=2, i=PACK),
             w4s_raw[:].rearrange("p a (b q i) -> p (a b) i q", b=2, i=PACK),
         )
         for c in range(2):
             nc.vector.tensor_copy(v_w[1][c][:], tab_w[1][:].indirect(list1[:, 32 * c : 32 * (c + 1)]))
+        for t in range(4, 8):
+            nc.sync.dma_start(z[t][:], plot_rows[t // PACK, t % PACK])
+        nc.sync.dma_start(w2_raw[:], w2.rearrange("(b p i) n -> p b i n", b=2, i=PACK))
 
         def features(t):
+            factor = gain_t[:, t // PACK, t % PACK : t % PACK + 1]
             for c in range(2):
                 cols = slice(BANK * c, BANK * (c + 1))
-                acc = psum.tile([P, BANK], F32, name="acc", tag="acc", bufs=4)
+                acc = psum.tile([P, BANK], F32, name="acc", tag="acc", bufs=4, offset=0)
                 for a in range(2):
                     nc.tensor.matmul_mx(
                         out=acc[:],
@@ -112,41 +123,46 @@ def tile_list_barley_duplicate_overlap_kernel(
                         stop=(a == 1),
                     )
                 nc.vector.tensor_tensor(z[t][:, cols], acc[:], z[t][:, cols], ALU.add)
-            nc.scalar.activation(z[t][:], z[t][:], ACT.Tanh)
-            nc.scalar.activation(h[t][:], z[t][:], ACT.Copy, scale=gain_t[:, t // PACK, t % PACK : t % PACK + 1])
+                if t == 0:
+                    nc.scalar.activation(z[t][:, cols], z[t][:, cols], ACT.Tanh)
+                    nc.scalar.activation(h[t][:, cols], z[t][:, cols], ACT.Copy, scale=factor)
+            if t > 0:
+                nc.scalar.activation(z[t][:], z[t][:], ACT.Tanh)
+                nc.scalar.activation(h[t][:], z[t][:], ACT.Copy, scale=factor)
 
-        def pick(t, m0, w, x_rows, last):
-            b, i = divmod(t, PACK)
+        def gather(t, m0, w, xa, xb):
             lists = slice(m0 // 16, (m0 + w) // 16)
-            xa = ring.tile([P, w], F32, name="xa", tag="xa", align_bytes=64)
-            xb = ring.tile([P, w], F32, name="xb", tag="xb", align_bytes=64)
-            lo = ring.tile([P, w], F32, name="lo", tag="lo", align_bytes=64)
-            nc.vector.tensor_tensor(xa[:], h[t][:].indirect(list2[:, lists]), wga_t[:, m0 : m0 + w], ALU.mult)
-            nc.vector.tensor_tensor(xb[:], h[t][:].indirect(list3[:, lists]), wgb_t[:, m0 : m0 + w], ALU.mult)
-            nc.vector.tensor_tensor(lo[:], xa[:], xb[:], ALU.min)
-            if last:
-                nc.vector.tensor_scalar(x_rows[:, i, :], lo[:], gv_t[:, b, i : i + 1], None, ALU.mult)
-            else:
-                nc.scalar.activation(x_rows[:, i, :], lo[:], ACT.Copy, scale=gv_t[:, b, i : i + 1])
+            nc.vector.tensor_tensor(xa, h[t][:].indirect(list2[:, lists]), wga_t[:, m0 : m0 + w], ALU.mult)
+            nc.vector.tensor_tensor(xb, h[t][:].indirect(list3[:, lists]), wgb_t[:, m0 : m0 + w], ALU.mult)
 
-        def weave(copy, rows, w, codes, scales):
-            woven = ring.tile([P, w, PACK], BF16, name="woven", tag="woven", align_bytes=64)
-            copy(
-                woven[:].rearrange("p (c j) i -> p c i j", j=4),
-                rows.rearrange("p i (c j) -> p c i j", j=4),
-            )
+        def pick(t, w, x_rows):
+            b, i = divmod(t, PACK)
+            if t == HELD:
+                xa = twice.tile([P, w], F32, name="xa_held", offset=67 * KB, align_bytes=64)
+                xb = twice.tile([P, w], F32, name="xb_held", offset=72 * KB, align_bytes=64)
+            else:
+                xa = ring.tile([P, w], F32, name="xa", tag="xa", align_bytes=64)
+                xb = ring.tile([P, w], F32, name="xb", tag="xb", align_bytes=64)
+            lo = ring.tile([P, w], F32, name="lo", tag="lo", align_bytes=64)
+            gather(t, 0, w, xa[:], xb[:])
+            nc.vector.tensor_tensor(lo[:], xa[:], xb[:], ALU.min)
+            nc.scalar.activation(x_rows[:, i, :], lo[:], ACT.Copy, scale=gv_t[:, b, i : i + 1])
+
+        def quantize(woven, codes, scales):
             nc.vector.quantize_mx(out=codes.bitcast(FP8X4), scales=scales, in_=woven[:].rearrange("p w i -> p (w i)"))
 
-        banks = {}
-        for m0, w in CHUNKS:
-            per = BANK // w
-            for g in range(4 // per):
-                banks[m0, g] = psum.tile([P, per, w], F32, name="sum%d_%d" % (m0, g))
+        def weave(rows, w, name, at):
+            woven = twice.tile([P, w, PACK], BF16, name=name, offset=at * KB, align_bytes=64)
+            nc.scalar.copy(woven[:].rearrange("p (c j) i -> p c i j", j=4), rows.rearrange("p i (c j) -> p c i j", j=4))
+            return woven
 
-        def product(b, m0, w):
-            per = BANK // w
+        banks = {}
+
+        def product(b, m0, w, per):
             for n in range(4):
                 g, s = divmod(n, per)
+                if b == 0 and s == 0:
+                    banks[m0, g] = psum.tile([P, per, w], F32, name="sum%d_%d" % (m0, g), offset=2 * KB * (7 - len(banks)))
                 nc.tensor.matmul_mx(
                     out=banks[m0, g][:, s, :],
                     lhsT=w2_w[b][:, P * n : P * (n + 1)].bitcast(FP8X4),
@@ -159,31 +175,51 @@ def tile_list_barley_duplicate_overlap_kernel(
 
         out_rows = out.rearrange("(n p) m -> p n m", p=P)
 
-        def store(m0, w):
-            per = BANK // w
-            for g in range(4 // per):
-                res = keep.tile([P, per, w], F32, name="res%d_%d" % (m0, g), align_bytes=64)
-                nc.scalar.copy(res[:], banks[m0, g][:])
-                nc.sync.dma_start(out_rows[:, per * g : per * (g + 1), m0 : m0 + w], res[:])
+        def store(m0, w, per, g, copy, queue):
+            res = keep.tile([P, per, w], F32, name="res%d_%d" % (m0, g), align_bytes=64)
+            copy(res[:], banks[m0, g][:])
+            queue.dma_start(out_rows[:, per * g : per * (g + 1), m0 : m0 + w], res[:])
 
         x0 = keep.tile([P, PACK, M], BF16, name="x0", align_bytes=64)
+        x1 = keep.tile([P, PACK, FIRST], BF16, name="x1", align_bytes=64)
         features(0)
         features(1)
         for t in range(PACK):
             features(t + 2)
-            pick(t, 0, M, x0, False)
+            pick(t, M, x0)
         features(6)
         features(7)
-        weave(nc.scalar.copy, x0[:], M, x_w[0][:], x_s[0][:])
+        x0_woven = weave(x0[:], M, "x0_woven", 64)
+        w2_woven = [weave(w2_raw[:, b, :, :], N, "w2_woven%d" % b, 68 + 4 * b) for b in range(2)]
+        pick(PACK, FIRST, x1)
+        quantize(x0_woven, x_w[0][:], x_s[0][:])
         for b in range(2):
-            weave(nc.scalar.copy, w2_raw[b][:], N, w2_w[b][:], w2_s[b][:])
-        for m0, w in CHUNKS:
-            product(0, m0, w)
-        for m0, w in CHUNKS:
-            last = m0 == CHUNKS[-1][0]
-            x1 = keep.tile([P, PACK, w], BF16, name="x1_%d" % m0, align_bytes=64)
-            for t in range(PACK, 2 * PACK):
-                pick(t, m0, w, x1, last)
-            weave(nc.vector.tensor_copy if last else nc.scalar.copy, x1[:], w, x_w[1][:, m0 : m0 + w], x_s[1][:, m0 : m0 + w])
-            product(1, m0, w)
-            store(m0, w)
+            quantize(w2_woven[b], w2_w[b][:], w2_s[b][:])
+        for m0, w, per in SUMS:
+            product(0, m0, w, per)
+        for t in range(PACK + 1, 2 * PACK):
+            pick(t, FIRST, x1)
+        x1_woven = weave(x1[:], FIRST, "x1_woven", 76)
+
+        rest = M - FIRST
+        xa = keep.tile([P, PACK, rest], F32, name="xa_rest", align_bytes=64)
+        xb = keep.tile([P, PACK, rest], F32, name="xb_rest", align_bytes=64)
+        lo = twice.tile([P, PACK, rest], F32, name="lo_rest", offset=76 * KB, align_bytes=64)
+        rest_woven = keep.tile([P, rest, PACK], BF16, name="rest_woven", align_bytes=64)
+        for i in range(PACK):
+            gather(PACK + i, FIRST, rest, xa[:, i, :], xb[:, i, :])
+            if i == 3:
+                quantize(x1_woven, x_w[1][:, 0:FIRST], x_s[1][:, 0:FIRST])
+        nc.vector.tensor_tensor(lo[:], xa[:], xb[:], ALU.min)
+        nc.vector.tensor_tensor(
+            rest_woven[:], lo[:].rearrange("p i m -> p m i"), gv_t[:, 1:2, :].to_broadcast([P, rest, PACK]), ALU.mult
+        )
+        for m0, w, per in SUMS[:2]:
+            product(1, m0, w, per)
+            for g in range(4 // per):
+                store(m0, w, per, g, nc.scalar.copy, nc.sync)
+        quantize(rest_woven, x_w[1][:, FIRST:M], x_s[1][:, FIRST:M])
+        m0, w, per = SUMS[2]
+        product(1, m0, w, per)
+        store(m0, w, per, 0, nc.vector.tensor_copy, nc.sync)
+        store(m0, w, per, 1, nc.scalar.copy, nc.scalar)

@@ -1,6 +1,7 @@
 from contextlib import ExitStack
 
 import concourse.mybir as mybir
+from concourse.masks import make_identity
 
 K, T, S, M, H, N = 1024, 4096, 1024, 512, 1024, 512
 FLOPS = 2 * K * H * S + 2 * H * N * M
@@ -20,7 +21,8 @@ P = 128
 PACK = 4
 BANK = 512
 FIRST = 384
-HELD = 5
+TURNED = (2, 4, 6)
+HELD = 7
 SUMS = ((0, 256, 2), (256, 128, 4), (384, 128, 2))
 
 
@@ -60,6 +62,8 @@ def tile_list_barley_duplicate_overlap_kernel(
         x_s = [keep.tile([P, M], U8, name="x_s%d" % b, align_bytes=64) for b in range(2)]
 
         nc.gpsimd.memset(w4s_raw[:].rearrange("p a c -> p (a c)").bitcast(I32), 0)
+        ident = keep.tile([P, P], F32, name="ident", align_bytes=64)
+        make_identity(nc, ident[:])
         nc.sync.dma_start(list1[:], offs)
         for q in range(4):
             nc.sync.dma_start(tab_s[32 * q + 24 : 32 * q + 32, :].bitcast(I32), tab_scales[:, 4 * q : 4 * q + 4, :].bitcast(I32))
@@ -122,11 +126,30 @@ def tile_list_barley_duplicate_overlap_kernel(
                         start=(a == 0),
                         stop=(a == 1),
                     )
+                if t in TURNED:
+                    y = ring.tile([P, BANK], F32, name="y", tag="y", align_bytes=64)
+                    nc.scalar.copy(y[:], acc[:])
+                    z_turned = psum.tile([P, 4, P], F32, name="z_turned", tag="z_turned", bufs=2, offset=8 * KB)
+                    for u in range(4):
+                        nc.tensor.matmul(
+                            z_turned[:, u, :], z[t][:, BANK * c + P * u : BANK * c + P * (u + 1)], ident[:],
+                            start=True, stop=False, is_transpose=True,
+                        )
+                        nc.tensor.matmul(
+                            z_turned[:, u, :], y[:, P * u : P * (u + 1)], ident[:], start=False, stop=True, is_transpose=True
+                        )
+                    t_turned = ring.tile([P, 4, P], F32, name="t_turned", tag="t_turned", align_bytes=64)
+                    nc.scalar.activation(t_turned[:], z_turned[:], ACT.Tanh)
+                    t_back = psum.tile([P, 4, P], F32, name="t_back", tag="t_back", bufs=2, offset=12 * KB)
+                    for u in range(4):
+                        nc.tensor.transpose(t_back[:, u, :], t_turned[:, u, :], ident[:])
+                    nc.scalar.activation(h[t][:, cols], t_back[:].rearrange("p u j -> p (u j)"), ACT.Copy, scale=factor)
+                    continue
                 nc.vector.tensor_tensor(z[t][:, cols], acc[:], z[t][:, cols], ALU.add)
                 if t == 0:
                     nc.scalar.activation(z[t][:, cols], z[t][:, cols], ACT.Tanh)
                     nc.scalar.activation(h[t][:, cols], z[t][:, cols], ACT.Copy, scale=factor)
-            if t > 0:
+            if t > 0 and t not in TURNED:
                 nc.scalar.activation(z[t][:], z[t][:], ACT.Tanh)
                 nc.scalar.activation(h[t][:], z[t][:], ACT.Copy, scale=factor)
 
@@ -143,7 +166,7 @@ def tile_list_barley_duplicate_overlap_kernel(
             else:
                 xa = ring.tile([P, w], F32, name="xa", tag="xa", align_bytes=64)
                 xb = ring.tile([P, w], F32, name="xb", tag="xb", align_bytes=64)
-            lo = ring.tile([P, w], F32, name="lo", tag="lo", align_bytes=64)
+            lo = keep.tile([P, w], F32, name="lo%d" % t, align_bytes=64)
             gather(t, 0, w, xa[:], xb[:])
             nc.vector.tensor_tensor(lo[:], xa[:], xb[:], ALU.min)
             nc.scalar.activation(x_rows[:, i, :], lo[:], ACT.Copy, scale=gv_t[:, b, i : i + 1])
@@ -151,9 +174,9 @@ def tile_list_barley_duplicate_overlap_kernel(
         def quantize(woven, codes, scales):
             nc.vector.quantize_mx(out=codes.bitcast(FP8X4), scales=scales, in_=woven[:].rearrange("p w i -> p (w i)"))
 
-        def weave(rows, w, name, at):
+        def weave(copy, rows, w, name, at):
             woven = twice.tile([P, w, PACK], BF16, name=name, offset=at * KB, align_bytes=64)
-            nc.scalar.copy(woven[:].rearrange("p (c j) i -> p c i j", j=4), rows.rearrange("p i (c j) -> p c i j", j=4))
+            copy(woven[:].rearrange("p (c j) i -> p c i j", j=4), rows.rearrange("p i (c j) -> p c i j", j=4))
             return woven
 
         banks = {}
@@ -182,24 +205,22 @@ def tile_list_barley_duplicate_overlap_kernel(
 
         x0 = keep.tile([P, PACK, M], BF16, name="x0", align_bytes=64)
         x1 = keep.tile([P, PACK, FIRST], BF16, name="x1", align_bytes=64)
-        features(0)
-        features(1)
+        for t in range(2 * PACK):
+            features(t)
         for t in range(PACK):
-            features(t + 2)
             pick(t, M, x0)
-        features(6)
-        features(7)
-        x0_woven = weave(x0[:], M, "x0_woven", 64)
-        w2_woven = [weave(w2_raw[:, b, :, :], N, "w2_woven%d" % b, 68 + 4 * b) for b in range(2)]
-        pick(PACK, FIRST, x1)
+        x0_woven = weave(nc.scalar.copy, x0[:], M, "x0_woven", 64)
+        w2_woven = [weave(nc.scalar.copy, w2_raw[:, b, :, :], N, "w2_woven%d" % b, 68 + 4 * b) for b in range(2)]
+        for t in range(PACK, HELD):
+            pick(t, FIRST, x1)
         quantize(x0_woven, x_w[0][:], x_s[0][:])
         for b in range(2):
             quantize(w2_woven[b], w2_w[b][:], w2_s[b][:])
         for m0, w, per in SUMS:
             product(0, m0, w, per)
-        for t in range(PACK + 1, 2 * PACK):
+        for t in range(HELD, 2 * PACK):
             pick(t, FIRST, x1)
-        x1_woven = weave(x1[:], FIRST, "x1_woven", 76)
+        x1_woven = weave(nc.scalar.copy, x1[:], FIRST, "x1_woven", 76)
 
         rest = M - FIRST
         xa = keep.tile([P, PACK, rest], F32, name="xa_rest", align_bytes=64)

@@ -64,6 +64,8 @@ def tile_list_barley_duplicate_overlap_kernel(
         nc.gpsimd.memset(w4s_raw[:].rearrange("p a c -> p (a c)").bitcast(I32), 0)
         ident = keep.tile([P, P], F32, name="ident", align_bytes=64)
         make_identity(nc, ident[:])
+        warm = keep.tile([P, 1], F32, name="warm")
+        nc.scalar.activation(warm[:], ident[:, 0:1], ACT.Tanh)
         nc.sync.dma_start(list1[:], offs)
         for q in range(4):
             nc.sync.dma_start(tab_s[32 * q + 24 : 32 * q + 32, :].bitcast(I32), tab_scales[:, 4 * q : 4 * q + 4, :].bitcast(I32))

@@ -20,10 +20,21 @@ ACT = mybir.ActivationFunctionType
 P = 128
 PACK = 4
 BANK = 512
-FIRST = 384
+KB = 1024
+TILES = H // P
+QUADRANTS = (0, 2, 1, 3)
+STAGED = 24
+
 TURNED = (2, 4, 6)
-HELD = 7
-SUMS = ((0, 256, 2), (256, 128, 4), (384, 128, 2))
+GAIN_ON_VECTOR = (0, 1)
+FIRST = 384
+REST = M - FIRST
+SUMS = ((0, 256, 2), (256, 128, 4), (FIRST, REST, 2))
+
+AT_TAB1 = 2 * KB
+AT_TAB0 = 34 * KB
+AT_W4 = 56 * KB
+AT_WOVEN = 64 * KB
 
 
 def tile_list_barley_duplicate_overlap_kernel(
@@ -36,82 +47,120 @@ def tile_list_barley_duplicate_overlap_kernel(
         psum = ctx.enter_context(tc.psum_pool(name="psum", bufs=1))
         twice = ctx.enter_context(tc.tile_pool(name="twice", bufs=1))
 
+        def placed(name, shape, dtype, offset):
+            return twice.tile(shape, dtype, name=name, offset=offset, align_bytes=64)
+
         list1 = keep.tile([P, S // 16], U16, name="list1")
         list2 = keep.tile([P, M // 16], U16, name="list2")
         list3 = keep.tile([P, M // 16], U16, name="list3")
-        KB = 1024
-        tab_s = twice.tile([P, T], U8, name="tab_s", offset=0)
-        tab_w = [twice.tile([P, T], U32, name="tab_w%d" % a, offset=at * KB) for a, at in enumerate((38, 4))]
+        tab_s = keep.tile([P, T], U8, name="tab_s", align_bytes=64)
         v_w = [[keep.tile([P, BANK], U32, name="v_w%d%d" % (a, c), align_bytes=64) for c in range(2)] for a in range(2)]
-        v_sg = keep.tile([P, S], U8, name="v_sg", align_bytes=64)
+        v_staged = keep.tile([P, S], U8, name="v_staged", align_bytes=64)
         v_s = [keep.tile([P, S], U8, name="v_s%d" % a, align_bytes=64) for a in range(2)]
-        w4_raw = twice.tile([P, 2, 2 * H], U8, name="w4_raw", offset=84 * KB)
-        w4_w = twice.tile([P, 2, 2 * H], U8, name="w4_w", offset=45 * KB, align_bytes=64)
         w4s_raw = keep.tile([P, 2, H], U8, name="w4s_raw", align_bytes=64)
-        w4_s = twice.tile([P, 2, H], U8, name="w4_s", offset=0, align_bytes=64)
-        gain_t = twice.tile([P, 2, PACK], F32, name="gain_t", offset=53 * KB + 64)
-        gv_t = twice.tile([P, 2, PACK], F32, name="gv_t", offset=53 * KB)
-        wga_t = twice.tile([P, M], F32, name="wga_t", offset=49 * KB)
-        wgb_t = twice.tile([P, M], F32, name="wgb_t", offset=51 * KB)
-        z = [twice.tile([P, S], F32, name="z%d" % t, offset=at * KB) for t, at in enumerate((37, 41, 81, 85, 2, 6, 10, 14))]
-        h = [keep.tile([P, S], F32, name="h%d" % t, align_bytes=64) for t in range(8)]
-        w2_raw = twice.tile([P, 2, PACK, N], F32, name="w2_raw", offset=18 * KB)
+        h = [keep.tile([P, S], F32, name="h%d" % t, align_bytes=64) for t in range(TILES)]
         w2_w = [keep.tile([P, N], U32, name="w2_w%d" % b, align_bytes=64) for b in range(2)]
         w2_s = [keep.tile([P, N], U8, name="w2_s%d" % b, align_bytes=64) for b in range(2)]
         x_w = [keep.tile([P, M], U32, name="x_w%d" % b, align_bytes=64) for b in range(2)]
         x_s = [keep.tile([P, M], U8, name="x_s%d" % b, align_bytes=64) for b in range(2)]
+
+        tab_w = [placed("tab_w0", [P, T], U32, AT_TAB0), placed("tab_w1", [P, T], U32, AT_TAB1)]
+        w4_raw = placed("w4_raw", [P, 2, 2 * H], U8, AT_W4)
+        z_at = [AT_TAB0 - 2 * KB, AT_TAB0 + 2 * KB, AT_W4 - 3 * KB, AT_W4 + 2 * KB]
+        z_at = z_at + [AT_TAB1 - 2 * KB + 4 * KB * u for u in range(4)]
+        z = [placed("z%d" % t, [P, S], F32, z_at[t]) for t in range(TILES)]
+        w2_raw = placed("w2_raw", [P, 2, PACK, N], F32, AT_TAB1 + 14 * KB)
+        w4_w = placed("w4_w", [P, 2, 2 * H], U8, AT_TAB0 + 6 * KB)
+        wga_t = placed("wga_t", [P, M], F32, AT_TAB0 + 10 * KB)
+        wgb_t = placed("wgb_t", [P, M], F32, AT_TAB0 + 12 * KB)
+        gain_t = placed("gain_t", [P, 2, PACK], F32, AT_TAB0 + 14 * KB)
+        w4_s = placed("w4_s", [P, 2, H], U8, AT_TAB0 + 15 * KB)
+        gv_t = placed("gv_t", [P, 2, PACK], F32, AT_W4 + KB)
 
         nc.gpsimd.memset(w4s_raw[:].rearrange("p a c -> p (a c)").bitcast(I32), 0)
         ident = keep.tile([P, P], F32, name="ident", align_bytes=64)
         make_identity(nc, ident[:])
         warm = keep.tile([P, 1], F32, name="warm")
         nc.scalar.activation(warm[:], ident[:, 0:1], ACT.Tanh)
+
         nc.sync.dma_start(list1[:], offs)
-        for q in range(4):
-            nc.sync.dma_start(tab_s[32 * q + 24 : 32 * q + 32, :].bitcast(I32), tab_scales[:, 4 * q : 4 * q + 4, :].bitcast(I32))
+        for q in QUADRANTS:
+            nc.sync.dma_start(
+                tab_s[32 * q + STAGED : 32 * q + 32, :].bitcast(I32), tab_scales[:, 4 * q : 4 * q + 4, :].bitcast(I32)
+            )
         nc.sync.dma_start(tab_w[0][:].bitcast(I32), tab_words[0].rearrange("p t i -> p (t i)").bitcast(I32))
         nc.sync.dma_start(w4_raw[:].bitcast(I32), w4_words.rearrange("a p c -> p a c").bitcast(I32))
-        for q in range(4):
+        for q in QUADRANTS:
             nc.sync.dma_start(
                 w4s_raw[32 * q : 32 * q + 4, :, :].bitcast(I32),
-                w4_scales[:, 4 * q : 4 * q + 4, :].rearrange("a r c -> r a c").bitcast(I32),
+                w4_scales[:, 4 * q : 4 * q + 4, :].rearrange("a s c -> s a c").bitcast(I32),
             )
         nc.sync.dma_start(tab_w[1][:].bitcast(I32), tab_words[1].rearrange("p t i -> p (t i)").bitcast(I32))
-        plot_rows = plot.rearrange("(b p i) j -> b i p j", b=2, i=PACK)
         nc.sync.dma_start(list2[:], offs2)
         nc.sync.dma_start(list3[:], offs3)
 
         for q in range(4):
-            nc.vector.memset(tab_s[32 * q : 32 * q + 24, :].bitcast(I32), 0)
+            nc.vector.memset(tab_s[32 * q : 32 * q + STAGED, :].bitcast(I32), 0)
         for a in range(2):
             nc.vector.memset(v_s[a][96:128, :].bitcast(I32), 0)
 
-        nc.vector.tensor_copy(v_sg[:], tab_s[:].indirect(list1[:]))
+        nc.vector.tensor_copy(v_staged[:], tab_s[:].indirect(list1[:]))
         for a in range(2):
-            nc.scalar.dma_start(v_s[a][0:100, :].bitcast(I32), v_sg[24 + 4 * a : 124 + 4 * a, :].bitcast(I32))
-        for c in range(2):
-            nc.vector.tensor_copy(v_w[0][c][:], tab_w[0][:].indirect(list1[:, 32 * c : 32 * (c + 1)]))
-        for t in range(2):
-            nc.sync.dma_start(z[t][:], plot_rows[t // PACK, t % PACK])
+            down = STAGED + 4 * a
+            nc.scalar.dma_start(v_s[a][0:100, :].bitcast(I32), v_staged[down : down + 100, :].bitcast(I32))
+
+        def gather_words(a):
+            for c in range(2):
+                nc.vector.tensor_copy(v_w[a][c][:], tab_w[a][:].indirect(list1[:, 32 * c : 32 * (c + 1)]))
+
+        plot_rows = plot.rearrange("(b p i) j -> b i p j", b=2, i=PACK)
+
+        def load_plot(tiles):
+            for t in tiles:
+                nc.sync.dma_start(z[t][:], plot_rows[t // PACK, t % PACK])
+
+        gather_words(0)
+        load_plot(range(0, 2))
         nc.sync.dma_start(gain_t[:], gain.rearrange("(b p i) -> p b i", b=2, i=PACK))
         nc.sync.dma_start(wga_t[:], wga)
         nc.sync.dma_start(wgb_t[:], wgb)
-        nc.sync.dma_start(gv_t[:], gv.rearrange("(b p i) -> p b i", b=2, i=PACK))
         nc.vector.tensor_copy(
             w4_w[:].bitcast(U16).rearrange("p a (b i q) -> p (a b) i q", b=2, i=PACK),
             w4_raw[:].bitcast(U16).rearrange("p a (b q i) -> p (a b) i q", b=2, i=PACK),
         )
-        for t in range(2, 4):
-            nc.sync.dma_start(z[t][:], plot_rows[t // PACK, t % PACK])
+        load_plot(range(2, 4))
+        nc.sync.dma_start(gv_t[:], gv.rearrange("(b p i) -> p b i", b=2, i=PACK))
         nc.vector.tensor_copy(
             w4_s[:].rearrange("p a (b i q) -> p (a b) i q", b=2, i=PACK),
             w4s_raw[:].rearrange("p a (b q i) -> p (a b) i q", b=2, i=PACK),
         )
-        for c in range(2):
-            nc.vector.tensor_copy(v_w[1][c][:], tab_w[1][:].indirect(list1[:, 32 * c : 32 * (c + 1)]))
-        for t in range(4, 8):
-            nc.sync.dma_start(z[t][:], plot_rows[t // PACK, t % PACK])
+        gather_words(1)
+        load_plot(range(4, TILES))
         nc.sync.dma_start(w2_raw[:], w2.rearrange("(b p i) n -> p b i n", b=2, i=PACK))
+
+        def finish_turned(t, cols, acc, factor):
+            y = ring.tile([P, BANK], F32, name="y", tag="y", align_bytes=64)
+            nc.scalar.copy(y[:], acc[:])
+            z_turned = psum.tile([P, 4, P], F32, name="z_turned", tag="z_turned", bufs=2, offset=8 * KB)
+            for u in range(4):
+                plot_block = z[t][:, cols.start + P * u : cols.start + P * (u + 1)]
+                nc.tensor.matmul(z_turned[:, u, :], plot_block, ident[:], start=True, stop=False, is_transpose=True)
+                nc.tensor.matmul(
+                    z_turned[:, u, :], y[:, P * u : P * (u + 1)], ident[:], start=False, stop=True, is_transpose=True
+                )
+            t_turned = ring.tile([P, 4, P], F32, name="t_turned", tag="t_turned", align_bytes=64)
+            nc.scalar.activation(t_turned[:], z_turned[:], ACT.Tanh)
+            t_back = psum.tile([P, 4, P], F32, name="t_back", tag="t_back", bufs=2, offset=12 * KB)
+            for u in range(4):
+                nc.tensor.transpose(t_back[:, u, :], t_turned[:, u, :], ident[:])
+            nc.scalar.activation(h[t][:, cols], t_back[:].rearrange("p u j -> p (u j)"), ACT.Copy, scale=factor)
+
+        def tanh_and_gain(t, cols, factor):
+            nc.scalar.activation(z[t][:, cols], z[t][:, cols], ACT.Tanh)
+            if t in GAIN_ON_VECTOR:
+                nc.vector.tensor_scalar(h[t][:, cols], z[t][:, cols], factor, None, ALU.mult)
+            else:
+                nc.scalar.activation(h[t][:, cols], z[t][:, cols], ACT.Copy, scale=factor)
 
         def features(t):
             factor = gain_t[:, t // PACK, t % PACK : t % PACK + 1]
@@ -129,62 +178,43 @@ def tile_list_barley_duplicate_overlap_kernel(
                         stop=(a == 1),
                     )
                 if t in TURNED:
-                    y = ring.tile([P, BANK], F32, name="y", tag="y", align_bytes=64)
-                    nc.scalar.copy(y[:], acc[:])
-                    z_turned = psum.tile([P, 4, P], F32, name="z_turned", tag="z_turned", bufs=2, offset=8 * KB)
-                    for u in range(4):
-                        nc.tensor.matmul(
-                            z_turned[:, u, :], z[t][:, BANK * c + P * u : BANK * c + P * (u + 1)], ident[:],
-                            start=True, stop=False, is_transpose=True,
-                        )
-                        nc.tensor.matmul(
-                            z_turned[:, u, :], y[:, P * u : P * (u + 1)], ident[:], start=False, stop=True, is_transpose=True
-                        )
-                    t_turned = ring.tile([P, 4, P], F32, name="t_turned", tag="t_turned", align_bytes=64)
-                    nc.scalar.activation(t_turned[:], z_turned[:], ACT.Tanh)
-                    t_back = psum.tile([P, 4, P], F32, name="t_back", tag="t_back", bufs=2, offset=12 * KB)
-                    for u in range(4):
-                        nc.tensor.transpose(t_back[:, u, :], t_turned[:, u, :], ident[:])
-                    nc.scalar.activation(h[t][:, cols], t_back[:].rearrange("p u j -> p (u j)"), ACT.Copy, scale=factor)
-                    continue
-                nc.vector.tensor_tensor(z[t][:, cols], acc[:], z[t][:, cols], ALU.add)
-                if t == 0:
-                    nc.scalar.activation(z[t][:, cols], z[t][:, cols], ACT.Tanh)
-                    nc.scalar.activation(h[t][:, cols], z[t][:, cols], ACT.Copy, scale=factor)
+                    finish_turned(t, cols, acc, factor)
+                else:
+                    nc.vector.tensor_tensor(z[t][:, cols], acc[:], z[t][:, cols], ALU.add)
+                    if t == 0:
+                        tanh_and_gain(t, cols, factor)
             if t > 0 and t not in TURNED:
-                nc.scalar.activation(z[t][:], z[t][:], ACT.Tanh)
-                nc.scalar.activation(h[t][:], z[t][:], ACT.Copy, scale=factor)
+                tanh_and_gain(t, slice(0, S), factor)
 
-        def gather(t, m0, w, xa, xb):
-            lists = slice(m0 // 16, (m0 + w) // 16)
-            nc.vector.tensor_tensor(xa, h[t][:].indirect(list2[:, lists]), wga_t[:, m0 : m0 + w], ALU.mult)
-            nc.vector.tensor_tensor(xb, h[t][:].indirect(list3[:, lists]), wgb_t[:, m0 : m0 + w], ALU.mult)
+        def gather_pairs(t, m0, w, xa, xb):
+            entries = slice(m0 // 16, (m0 + w) // 16)
+            nc.vector.tensor_tensor(xa, h[t][:].indirect(list2[:, entries]), wga_t[:, m0 : m0 + w], ALU.mult)
+            nc.vector.tensor_tensor(xb, h[t][:].indirect(list3[:, entries]), wgb_t[:, m0 : m0 + w], ALU.mult)
 
-        def pick(t, w, x_rows):
+        def overlap(t, w, xa, xb, x_rows):
             b, i = divmod(t, PACK)
-            if t == HELD:
-                xa = twice.tile([P, w], F32, name="xa_held", offset=67 * KB, align_bytes=64)
-                xb = twice.tile([P, w], F32, name="xb_held", offset=72 * KB, align_bytes=64)
-            else:
-                xa = ring.tile([P, w], F32, name="xa", tag="xa", align_bytes=64)
-                xb = ring.tile([P, w], F32, name="xb", tag="xb", align_bytes=64)
-            lo = keep.tile([P, w], F32, name="lo%d" % t, align_bytes=64)
-            gather(t, 0, w, xa[:], xb[:])
-            nc.vector.tensor_tensor(lo[:], xa[:], xb[:], ALU.min)
-            nc.scalar.activation(x_rows[:, i, :], lo[:], ACT.Copy, scale=gv_t[:, b, i : i + 1])
+            low = keep.tile([P, w], F32, name="low%d" % t, align_bytes=64)
+            gather_pairs(t, 0, w, xa[:], xb[:])
+            nc.vector.tensor_tensor(low[:], xa[:], xb[:], ALU.min)
+            nc.scalar.activation(x_rows[:, i, :], low[:], ACT.Copy, scale=gv_t[:, b, i : i + 1])
+
+        def overlap_in_ring(t, w, x_rows):
+            xa = ring.tile([P, w], F32, name="xa", tag="xa", align_bytes=64)
+            xb = ring.tile([P, w], F32, name="xb", tag="xb", align_bytes=64)
+            overlap(t, w, xa, xb, x_rows)
+
+        def weave(rows, w, name, offset):
+            woven = placed(name, [P, w, PACK], BF16, offset)
+            nc.scalar.copy(woven[:].rearrange("p (c j) i -> p c i j", j=4), rows.rearrange("p i (c j) -> p c i j", j=4))
+            return woven
 
         def quantize(woven, codes, scales):
             nc.vector.quantize_mx(out=codes.bitcast(FP8X4), scales=scales, in_=woven[:].rearrange("p w i -> p (w i)"))
 
-        def weave(copy, rows, w, name, at):
-            woven = twice.tile([P, w, PACK], BF16, name=name, offset=at * KB, align_bytes=64)
-            copy(woven[:].rearrange("p (c j) i -> p c i j", j=4), rows.rearrange("p i (c j) -> p c i j", j=4))
-            return woven
-
         banks = {}
 
         def product(b, m0, w, per):
-            for n in range(4):
+            for n in range(N // P):
                 g, s = divmod(n, per)
                 if b == 0 and s == 0:
                     banks[m0, g] = psum.tile([P, per, w], F32, name="sum%d_%d" % (m0, g), offset=2 * KB * (7 - len(banks)))
@@ -207,42 +237,44 @@ def tile_list_barley_duplicate_overlap_kernel(
 
         x0 = keep.tile([P, PACK, M], BF16, name="x0", align_bytes=64)
         x1 = keep.tile([P, PACK, FIRST], BF16, name="x1", align_bytes=64)
-        for t in range(2 * PACK):
+        for t in range(TILES):
             features(t)
         for t in range(PACK):
-            pick(t, M, x0)
-        x0_woven = weave(nc.scalar.copy, x0[:], M, "x0_woven", 64)
-        w2_woven = [weave(nc.scalar.copy, w2_raw[:, b, :, :], N, "w2_woven%d" % b, 68 + 4 * b) for b in range(2)]
-        for t in range(PACK, HELD):
-            pick(t, FIRST, x1)
+            overlap_in_ring(t, M, x0)
+        x0_woven = weave(x0[:], M, "x0_woven", AT_WOVEN)
+        w2_woven = [weave(w2_raw[:, b, :, :], N, "w2_woven%d" % b, AT_WOVEN + 4 * KB * (b + 1)) for b in range(2)]
+        for t in range(PACK, TILES - 1):
+            overlap_in_ring(t, FIRST, x1)
         quantize(x0_woven, x_w[0][:], x_s[0][:])
         for b in range(2):
             quantize(w2_woven[b], w2_w[b][:], w2_s[b][:])
         for m0, w, per in SUMS:
             product(0, m0, w, per)
-        for t in range(HELD, 2 * PACK):
-            pick(t, FIRST, x1)
-        x1_woven = weave(nc.scalar.copy, x1[:], FIRST, "x1_woven", 76)
+        xa_last = placed("xa_last", [P, FIRST], F32, AT_WOVEN + 3 * KB)
+        xb_last = placed("xb_last", [P, FIRST], F32, AT_WOVEN + 8 * KB)
+        overlap(TILES - 1, FIRST, xa_last, xb_last, x1)
+        x1_woven = weave(x1[:], FIRST, "x1_woven", AT_WOVEN + 12 * KB)
 
-        rest = M - FIRST
-        xa = keep.tile([P, PACK, rest], F32, name="xa_rest", align_bytes=64)
-        xb = keep.tile([P, PACK, rest], F32, name="xb_rest", align_bytes=64)
-        lo = twice.tile([P, PACK, rest], F32, name="lo_rest", offset=76 * KB, align_bytes=64)
-        rest_woven = keep.tile([P, rest, PACK], BF16, name="rest_woven", align_bytes=64)
+        xa_rest = keep.tile([P, PACK, REST], F32, name="xa_rest", align_bytes=64)
+        xb_rest = keep.tile([P, PACK, REST], F32, name="xb_rest", align_bytes=64)
+        low_rest = placed("low_rest", [P, PACK, REST], F32, AT_WOVEN + 12 * KB)
+        rest_woven = keep.tile([P, REST, PACK], BF16, name="rest_woven", align_bytes=64)
         for i in range(PACK):
-            gather(PACK + i, FIRST, rest, xa[:, i, :], xb[:, i, :])
-            if i == 3:
-                quantize(x1_woven, x_w[1][:, 0:FIRST], x_s[1][:, 0:FIRST])
-        nc.vector.tensor_tensor(lo[:], xa[:], xb[:], ALU.min)
+            gather_pairs(PACK + i, FIRST, REST, xa_rest[:, i, :], xb_rest[:, i, :])
+        quantize(x1_woven, x_w[1][:, 0:FIRST], x_s[1][:, 0:FIRST])
+        nc.vector.tensor_tensor(low_rest[:], xa_rest[:], xb_rest[:], ALU.min)
         nc.vector.tensor_tensor(
-            rest_woven[:], lo[:].rearrange("p i m -> p m i"), gv_t[:, 1:2, :].to_broadcast([P, rest, PACK]), ALU.mult
+            rest_woven[:],
+            low_rest[:].rearrange("p i m -> p m i"),
+            gv_t[:, 1:2, :].to_broadcast([P, REST, PACK]),
+            ALU.mult,
         )
-        for m0, w, per in SUMS[:2]:
+        for m0, w, per in SUMS[:-1]:
             product(1, m0, w, per)
-            for g in range(4 // per):
+            for g in range(N // P // per):
                 store(m0, w, per, g, nc.scalar.copy, nc.sync)
         quantize(rest_woven, x_w[1][:, FIRST:M], x_s[1][:, FIRST:M])
-        m0, w, per = SUMS[2]
+        m0, w, per = SUMS[-1]
         product(1, m0, w, per)
         store(m0, w, per, 0, nc.vector.tensor_copy, nc.sync)
         store(m0, w, per, 1, nc.scalar.copy, nc.scalar)

from contextlib import ExitStack

import concourse.mybir as mybir
from concourse.masks import make_identity

K, T, S, M, H, N = 1024, 4096, 1024, 512, 1024, 512
FLOPS = 2 * K * H * S + 2 * H * N * M

F32 = mybir.dt.float32
BF16 = mybir.dt.bfloat16
I32 = mybir.dt.int32
U32 = mybir.dt.uint32
U16 = mybir.dt.uint16
U8 = mybir.dt.uint8
FP8X4 = mybir.dt.float8_e4m3fn_x4
FP4X4 = mybir.dt.float4_e2m1fn_x4
ALU = mybir.AluOpType
ACT = mybir.ActivationFunctionType

P = 128
PACK = 4
BANK = 512
KB = 1024
TILES = H // P
QUADRANTS = (0, 2, 1, 3)
STAGED = 24

TURNED = (2, 4, 6)
GAIN_ON_VECTOR = (0, 1)
FIRST = 384
REST = M - FIRST
SUMS = ((0, 256, 2), (256, 128, 4), (FIRST, REST, 2))

AT_TAB1 = 2 * KB
AT_TAB0 = 34 * KB
AT_W4 = 56 * KB
AT_WOVEN = 64 * KB


def tile_list_barley_duplicate_overlap_kernel(
    tc, tab_words, tab_scales, offs, w4_words, w4_scales, plot, gain, offs2, wga, offs3, wgb, gv, w2, out
):
    nc = tc.nc
    with ExitStack() as ctx:
        keep = ctx.enter_context(tc.tile_pool(name="keep", bufs=1))
        ring = ctx.enter_context(tc.tile_pool(name="ring", bufs=2))
        psum = ctx.enter_context(tc.psum_pool(name="psum", bufs=1))
        twice = ctx.enter_context(tc.tile_pool(name="twice", bufs=1))

        def placed(name, shape, dtype, offset):
            return twice.tile(shape, dtype, name=name, offset=offset, align_bytes=64)

        list1 = keep.tile([P, S // 16], U16, name="list1")
        list2 = keep.tile([P, M // 16], U16, name="list2")
        list3 = keep.tile([P, M // 16], U16, name="list3")
        tab_s = keep.tile([P, T], U8, name="tab_s", align_bytes=64)
        v_w = [[keep.tile([P, BANK], U32, name="v_w%d%d" % (a, c), align_bytes=64) for c in range(2)] for a in range(2)]
        v_staged = keep.tile([P, S], U8, name="v_staged", align_bytes=64)
        v_s = [keep.tile([P, S], U8, name="v_s%d" % a, align_bytes=64) for a in range(2)]
        w4s_raw = keep.tile([P, 2, H], U8, name="w4s_raw", align_bytes=64)
        h = [keep.tile([P, S], F32, name="h%d" % t, align_bytes=64) for t in range(TILES)]
        w2_w = [keep.tile([P, N], U32, name="w2_w%d" % b, align_bytes=64) for b in range(2)]
        w2_s = [keep.tile([P, N], U8, name="w2_s%d" % b, align_bytes=64) for b in range(2)]
        x_w = [keep.tile([P, M], U32, name="x_w%d" % b, align_bytes=64) for b in range(2)]
        x_s = [keep.tile([P, M], U8, name="x_s%d" % b, align_bytes=64) for b in range(2)]

        tab_w = [placed("tab_w0", [P, T], U32, AT_TAB0), placed("tab_w1", [P, T], U32, AT_TAB1)]
        w4_raw = placed("w4_raw", [P, 2, 2 * H], U8, AT_W4)
        z_at = [AT_TAB0 - 2 * KB, AT_TAB0 + 2 * KB, AT_W4 - 3 * KB, AT_W4 + 2 * KB]
        z_at = z_at + [AT_TAB1 - 2 * KB + 4 * KB * u for u in range(4)]
        z = [placed("z%d" % t, [P, S], F32, z_at[t]) for t in range(TILES)]
        w2_raw = placed("w2_raw", [P, 2, PACK, N], F32, AT_TAB1 + 14 * KB)
        w4_w = placed("w4_w", [P, 2, 2 * H], U8, AT_TAB0 + 6 * KB)
        wga_t = placed("wga_t", [P, M], F32, AT_TAB0 + 10 * KB)
        wgb_t = placed("wgb_t", [P, M], F32, AT_TAB0 + 12 * KB)
        gain_t = placed("gain_t", [P, 2, PACK], F32, AT_TAB0 + 14 * KB)
        w4_s = placed("w4_s", [P, 2, H], U8, AT_TAB0 + 15 * KB)
        gv_t = placed("gv_t", [P, 2, PACK], F32, AT_W4 + KB)

        nc.gpsimd.memset(w4s_raw[:].rearrange("p a c -> p (a c)").bitcast(I32), 0)
        ident = keep.tile([P, P], F32, name="ident", align_bytes=64)
        make_identity(nc, ident[:])
        warm = keep.tile([P, 1], F32, name="warm")
        nc.scalar.activation(warm[:], ident[:, 0:1], ACT.Tanh)

        nc.sync.dma_start(list1[:], offs)
        for q in QUADRANTS:
            nc.sync.dma_start(
                tab_s[32 * q + STAGED : 32 * q + 32, :].bitcast(I32), tab_scales[:, 4 * q : 4 * q + 4, :].bitcast(I32)
            )
        nc.sync.dma_start(tab_w[0][:].bitcast(I32), tab_words[0].rearrange("p t i -> p (t i)").bitcast(I32))
        nc.sync.dma_start(w4_raw[:].bitcast(I32), w4_words.rearrange("a p c -> p a c").bitcast(I32))
        for q in QUADRANTS:
            nc.sync.dma_start(
                w4s_raw[32 * q : 32 * q + 4, :, :].bitcast(I32),
                w4_scales[:, 4 * q : 4 * q + 4, :].rearrange("a s c -> s a c").bitcast(I32),
            )
        nc.sync.dma_start(tab_w[1][:].bitcast(I32), tab_words[1].rearrange("p t i -> p (t i)").bitcast(I32))
        nc.sync.dma_start(list2[:], offs2)
        nc.sync.dma_start(list3[:], offs3)

        for q in range(4):
            nc.vector.memset(tab_s[32 * q : 32 * q + STAGED, :].bitcast(I32), 0)
        for a in range(2):
            nc.vector.memset(v_s[a][96:128, :].bitcast(I32), 0)

        nc.vector.tensor_copy(v_staged[:], tab_s[:].indirect(list1[:]))
        for a in range(2):
            down = STAGED + 4 * a
            nc.scalar.dma_start(v_s[a][0:100, :].bitcast(I32), v_staged[down : down + 100, :].bitcast(I32))

        def gather_words(a):
            for c in range(2):
                nc.vector.tensor_copy(v_w[a][c][:], tab_w[a][:].indirect(list1[:, 32 * c : 32 * (c + 1)]))

        plot_rows = plot.rearrange("(b p i) j -> b i p j", b=2, i=PACK)

        def load_plot(tiles):
            for t in tiles:
                nc.sync.dma_start(z[t][:], plot_rows[t // PACK, t % PACK])

        gather_words(0)
        load_plot(range(0, 2))
        nc.sync.dma_start(gain_t[:], gain.rearrange("(b p i) -> p b i", b=2, i=PACK))
        nc.sync.dma_start(wga_t[:], wga)
        nc.sync.dma_start(wgb_t[:], wgb)
        nc.vector.tensor_copy(
            w4_w[:].bitcast(U16).rearrange("p a (b i q) -> p (a b) i q", b=2, i=PACK),
            w4_raw[:].bitcast(U16).rearrange("p a (b q i) -> p (a b) i q", b=2, i=PACK),
        )
        load_plot(range(2, 4))
        nc.sync.dma_start(gv_t[:], gv.rearrange("(b p i) -> p b i", b=2, i=PACK))
        nc.vector.tensor_copy(
            w4_s[:].rearrange("p a (b i q) -> p (a b) i q", b=2, i=PACK),
            w4s_raw[:].rearrange("p a (b q i) -> p (a b) i q", b=2, i=PACK),
        )
        gather_words(1)
        load_plot(range(4, TILES))
        nc.sync.dma_start(w2_raw[:], w2.rearrange("(b p i) n -> p b i n", b=2, i=PACK))

        def finish_turned(t, cols, acc, factor):
            y = ring.tile([P, BANK], F32, name="y", tag="y", align_bytes=64)
            nc.scalar.copy(y[:], acc[:])
            z_turned = psum.tile([P, 4, P], F32, name="z_turned", tag="z_turned", bufs=2, offset=8 * KB)
            for u in range(4):
                plot_block = z[t][:, cols.start + P * u : cols.start + P * (u + 1)]
                nc.tensor.matmul(z_turned[:, u, :], plot_block, ident[:], start=True, stop=False, is_transpose=True)
                nc.tensor.matmul(
                    z_turned[:, u, :], y[:, P * u : P * (u + 1)], ident[:], start=False, stop=True, is_transpose=True
                )
            t_turned = ring.tile([P, 4, P], F32, name="t_turned", tag="t_turned", align_bytes=64)
            nc.scalar.activation(t_turned[:], z_turned[:], ACT.Tanh)
            t_back = psum.tile([P, 4, P], F32, name="t_back", tag="t_back", bufs=2, offset=12 * KB)
            for u in range(4):
                nc.tensor.transpose(t_back[:, u, :], t_turned[:, u, :], ident[:])
            nc.scalar.activation(h[t][:, cols], t_back[:].rearrange("p u j -> p (u j)"), ACT.Copy, scale=factor)

        def tanh_and_gain(t, cols, factor):
            nc.scalar.activation(z[t][:, cols], z[t][:, cols], ACT.Tanh)
            if t in GAIN_ON_VECTOR:
                nc.vector.tensor_scalar(h[t][:, cols], z[t][:, cols], factor, None, ALU.mult)
            else:
                nc.scalar.activation(h[t][:, cols], z[t][:, cols], ACT.Copy, scale=factor)

        def features(t):
            factor = gain_t[:, t // PACK, t % PACK : t % PACK + 1]
            for c in range(2):
                cols = slice(BANK * c, BANK * (c + 1))
                acc = psum.tile([P, BANK], F32, name="acc", tag="acc", bufs=4, offset=0)
                for a in range(2):
                    nc.tensor.matmul_mx(
                        out=acc[:],
                        lhsT=w4_w[:, a, 2 * P * t : 2 * P * (t + 1)].bitcast(FP4X4),
                        lhsT_scale=w4_s[:, a, P * t : P * (t + 1)],
                        rhs=v_w[a][c][:].bitcast(FP8X4),
                        rhs_scale=v_s[a][:, cols],
                        start=(a == 0),
                        stop=(a == 1),
                    )
                if t in TURNED:
                    finish_turned(t, cols, acc, factor)
                else:
                    nc.vector.tensor_tensor(z[t][:, cols], acc[:], z[t][:, cols], ALU.add)
                    if t == 0:
                        tanh_and_gain(t, cols, factor)
            if t > 0 and t not in TURNED:
                tanh_and_gain(t, slice(0, S), factor)

        def gather_pairs(t, m0, w, xa, xb):
            entries = slice(m0 // 16, (m0 + w) // 16)
            nc.vector.tensor_tensor(xa, h[t][:].indirect(list2[:, entries]), wga_t[:, m0 : m0 + w], ALU.mult)
            nc.vector.tensor_tensor(xb, h[t][:].indirect(list3[:, entries]), wgb_t[:, m0 : m0 + w], ALU.mult)

        def overlap(t, w, xa, xb, x_rows):
            b, i = divmod(t, PACK)
            low = keep.tile([P, w], F32, name="low%d" % t, align_bytes=64)
            gather_pairs(t, 0, w, xa[:], xb[:])
            nc.vector.tensor_tensor(low[:], xa[:], xb[:], ALU.min)
            nc.scalar.activation(x_rows[:, i, :], low[:], ACT.Copy, scale=gv_t[:, b, i : i + 1])

        def overlap_in_ring(t, w, x_rows):
            xa = ring.tile([P, w], F32, name="xa", tag="xa", align_bytes=64)
            xb = ring.tile([P, w], F32, name="xb", tag="xb", align_bytes=64)
            overlap(t, w, xa, xb, x_rows)

        def weave(rows, w, name, offset):
            woven = placed(name, [P, w, PACK], BF16, offset)
            nc.scalar.copy(woven[:].rearrange("p (c j) i -> p c i j", j=4), rows.rearrange("p i (c j) -> p c i j", j=4))
            return woven

        def quantize(woven, codes, scales):
            nc.vector.quantize_mx(out=codes.bitcast(FP8X4), scales=scales, in_=woven[:].rearrange("p w i -> p (w i)"))

        banks = {}

        def product(b, m0, w, per):
            for n in range(N // P):
                g, s = divmod(n, per)
                if b == 0 and s == 0:
                    banks[m0, g] = psum.tile([P, per, w], F32, name="sum%d_%d" % (m0, g), offset=2 * KB * (7 - len(banks)))
                nc.tensor.matmul_mx(
                    out=banks[m0, g][:, s, :],
                    lhsT=w2_w[b][:, P * n : P * (n + 1)].bitcast(FP8X4),
                    lhsT_scale=w2_s[b][:, P * n : P * (n + 1)],
                    rhs=x_w[b][:, m0 : m0 + w].bitcast(FP8X4),
                    rhs_scale=x_s[b][:, m0 : m0 + w],
                    start=(b == 0 and s == 0),
                    stop=(b == 1 and s == per - 1),
                )

        out_rows = out.rearrange("(n p) m -> p n m", p=P)

        def store(m0, w, per, g, copy, queue):
            res = keep.tile([P, per, w], F32, name="res%d_%d" % (m0, g), align_bytes=64)
            copy(res[:], banks[m0, g][:])
            queue.dma_start(out_rows[:, per * g : per * (g + 1), m0 : m0 + w], res[:])

        x0 = keep.tile([P, PACK, M], BF16, name="x0", align_bytes=64)
        x1 = keep.tile([P, PACK, FIRST], BF16, name="x1", align_bytes=64)
        for t in range(TILES):
            features(t)
        for t in range(PACK):
            overlap_in_ring(t, M, x0)
        x0_woven = weave(x0[:], M, "x0_woven", AT_WOVEN)
        w2_woven = [weave(w2_raw[:, b, :, :], N, "w2_woven%d" % b, AT_WOVEN + 4 * KB * (b + 1)) for b in range(2)]
        for t in range(PACK, TILES - 1):
            overlap_in_ring(t, FIRST, x1)
        quantize(x0_woven, x_w[0][:], x_s[0][:])
        for b in range(2):
            quantize(w2_woven[b], w2_w[b][:], w2_s[b][:])
        for m0, w, per in SUMS:
            product(0, m0, w, per)
        xa_last = placed("xa_last", [P, FIRST], F32, AT_WOVEN + 3 * KB)
        xb_last = placed("xb_last", [P, FIRST], F32, AT_WOVEN + 8 * KB)
        overlap(TILES - 1, FIRST, xa_last, xb_last, x1)
        x1_woven = weave(x1[:], FIRST, "x1_woven", AT_WOVEN + 12 * KB)

        xa_rest = keep.tile([P, PACK, REST], F32, name="xa_rest", align_bytes=64)
        xb_rest = keep.tile([P, PACK, REST], F32, name="xb_rest", align_bytes=64)
        low_rest = placed("low_rest", [P, PACK, REST], F32, AT_WOVEN + 12 * KB)
        rest_woven = keep.tile([P, REST, PACK], BF16, name="rest_woven", align_bytes=64)
        for i in range(PACK):
            gather_pairs(PACK + i, FIRST, REST, xa_rest[:, i, :], xb_rest[:, i, :])
        quantize(x1_woven, x_w[1][:, 0:FIRST], x_s[1][:, 0:FIRST])
        nc.vector.tensor_tensor(low_rest[:], xa_rest[:], xb_rest[:], ALU.min)
        nc.vector.tensor_tensor(
            rest_woven[:],
            low_rest[:].rearrange("p i m -> p m i"),
            gv_t[:, 1:2, :].to_broadcast([P, REST, PACK]),
            ALU.mult,
        )
        for m0, w, per in SUMS[:-1]:
            product(1, m0, w, per)
            for g in range(N // P // per):
                store(m0, w, per, g, nc.scalar.copy, nc.sync)
        quantize(rest_woven, x_w[1][:, FIRST:M], x_s[1][:, FIRST:M])
        m0, w, per = SUMS[-1]
        product(1, m0, w, per)
        store(m0, w, per, 0, nc.vector.tensor_copy, nc.sync)
        store(m0, w, per, 1, nc.scalar.copy, nc.scalar)
